import numpy as np
import ml_dtypes


def mxq(x, axis, fmt="e4m3"):
    dtype, down = {"e4m3": (ml_dtypes.float8_e4m3fn, 7), "e5m2": (ml_dtypes.float8_e5m2, 14)}[fmt]
    v = np.moveaxis(np.asarray(x, np.float32).astype(ml_dtypes.bfloat16).astype(np.float64), axis, -1)
    blocks = v.reshape(v.shape[:-1] + (-1, 32))
    amax = np.abs(blocks).max(-1, keepdims=True)
    byte = np.maximum(np.where(amax > 0, np.frexp(amax)[1] - 1 + 127, 0) - down, 1)
    scale = np.exp2(byte - 127.0)
    codes = (blocks / scale).astype(np.float32).astype(dtype).astype(np.float64)
    return np.moveaxis((codes * scale).reshape(v.shape), -1, axis)


WIDE = False


def mx_kscale(k):
    if not WIDE:
        return np.ones(k)
    levels = np.array([10, -10, 5, -5, 0])
    if k % 512:
        return np.exp2(np.random.permutation(np.resize(levels, k // 32))).repeat(32)
    a = np.empty((k // 512, 16))
    for p in range(k // 512):
        a[p, :8] = np.random.permutation(np.resize(levels, 8))
        for g in range(8):
            far = levels[np.abs(levels - a[p, g]) >= 10]
            a[p, g + 8] = far[np.random.randint(len(far))]
    return np.exp2(a.ravel()).repeat(32)


def f64(x):
    return np.asarray(x).astype(np.float64)


def striped(idx):
    return np.tile(idx.reshape(-1, 16).T, (8, 1)).astype(np.uint16)


def unstriped(offs):
    return offs[:16].T.reshape(-1).astype(np.int64)


E2M1 = np.array([0.0, 0.5, 1.0, 1.5, 2.0, 3.0, 4.0, 6.0, -0.0, -0.5, -1.0, -1.5, -2.0, -3.0, -4.0, -6.0])


def pack_weight(w, fmt):
    k, n = w.shape
    w = f64(np.asarray(w, np.float32).astype(ml_dtypes.bfloat16)).reshape(k // 32, 32, n)
    amax = np.abs(w).max(1)
    if fmt == "e4m3":
        byte = np.frexp(amax)[1] - 1 + 127 - 7
    else:
        mant, ex = np.frexp(amax / 6.0)
        byte = np.where(mant > 0.5, ex, ex - 1) + 127
    byte = np.clip(np.where(amax > 0, byte, 1), 1, 254)
    scaled = (w * np.exp2(127.0 - byte)[:, None, :]).reshape(k, n).astype(np.float32)
    by_word = np.ascontiguousarray(scaled.reshape(k // 512, 128, 4, n).transpose(0, 1, 3, 2))
    if fmt == "e4m3":
        words = by_word.astype(ml_dtypes.float8_e4m3fn).view(np.uint8)
    else:
        c = by_word.astype(ml_dtypes.float4_e2m1fn).view(np.uint8) & 0xF
        words = (c[..., 0::2] | (c[..., 1::2] << 4)).reshape(k // 512, 128, 2 * n)
    return np.ascontiguousarray(words), np.ascontiguousarray(byte.astype(np.uint8).reshape(k // 512, 16, n))


def unpack_weight(words, scales, fmt):
    g, _, n = scales.shape
    words = np.ascontiguousarray(words).reshape(g, 128, n, -1)
    if fmt == "e4m3":
        vals = words.view(ml_dtypes.float8_e4m3fn).astype(np.float64)
    else:
        nib = np.empty((g, 128, n, 4), np.uint8)
        nib[..., 0::2] = words & 0xF
        nib[..., 1::2] = words >> 4
        vals = E2M1[nib]
    vals = vals * np.repeat(np.exp2(scales.astype(np.float64) - 127.0), 8, axis=1)[..., None]
    return vals.transpose(0, 1, 3, 2).reshape(g * 512, n)


def gelu(v):
    return 0.5 * v * (1.0 + np.tanh(np.sqrt(2.0 / np.pi) * (v + 0.044715 * v**3)))


K, H, N, T, S, P, P2 = 1536, 1024, 768, 4096, 1024, 512, 256

def setup_inputs():
    n = np.random.standard_normal
    s = mx_kscale(K)[:, None]
    u = mx_kscale(H)[:, None]
    tab_words, tab_scales = pack_weight(n((K, T)) * s, "e4m3")
    w2_words, w2_scales = pack_weight(n((H, N)) / np.sqrt(H) / u, "e2m1")
    return {
        "tab_words": tab_words, "tab_scales": tab_scales,
        "offs": striped(np.random.permutation(T)[:S]),
        "w1": (1.3 * n((K, H)) / np.sqrt(K) / s).astype(np.float32),
        "b1": (0.6 * n(H)).astype(np.float32),
        "gain": (np.exp(0.3 * n(H)) * u[:, 0]).astype(np.float32),
        "pos1": striped(np.random.permutation(S)[:P]),
        "pos2": striped(np.random.permutation(S)[:P]),
        "rest": np.exp(0.4 * n(H)).astype(np.float32),
        "strain": np.exp(0.4 * n(H)).astype(np.float32),
        "w2_words": w2_words, "w2_scales": w2_scales,
        "pos3": striped(np.random.permutation(P)[:P2]),
        "pos4": striped(np.random.permutation(P)[:P2]),
    }

def reference(tab_words, tab_scales, offs, w1, b1, gain, pos1, pos2, rest, strain,
              w2_words, w2_scales, pos3, pos4):
    v = unpack_weight(tab_words, tab_scales, "e4m3")[:, unstriped(offs)]
    d = (mxq(f64(w1), 0, "e4m3").T @ v) + f64(b1)[:, None]
    h = f64(gain)[:, None] * np.tanh(d)
    xr = f64(rest)[:, None] * h[:, unstriped(pos1)]
    xs = f64(strain)[:, None] * h[:, unstriped(pos2)]
    z = xr - xs
    w2 = unpack_weight(w2_words, w2_scales, "e2m1")
    y = w2.T @ mxq(z, 0, "e4m3")
    return np.maximum(y[:, unstriped(pos3)], y[:, unstriped(pos4)])

@@ -1,0 +1,199 @@
+from contextlib import ExitStack
+
+import concourse.mybir as mybir
+
+K, H, N, T, S, P1, P2 = 1536, 1024, 768, 4096, 1024, 512, 256
+FLOPS = 2 * K * H * S + 2 * H * N * P1
+
+F32 = mybir.dt.float32
+BF16 = mybir.dt.bfloat16
+I32 = mybir.dt.int32
+U32 = mybir.dt.uint32
+U16 = mybir.dt.uint16
+U8 = mybir.dt.uint8
+FP8X4 = mybir.dt.float8_e4m3fn_x4
+FP4X4 = mybir.dt.float4_e2m1fn_x4
+ALU = mybir.AluOpType
+ACT = mybir.ActivationFunctionType
+
+P = 128
+PACK = 4
+PASS = P * PACK
+BANK = 512
+K_PASSES = K // PASS
+H_PASSES = H // PASS
+HALVES = S // BANK
+N_TILES = N // P
+
+
+def tile_list_ewe_posture_contrast_kernel(
+    tc, tab_words, tab_scales, offs, w1, b1, gain, pos1, pos2, rest, strain,
+    w2_words, w2_scales, pos3, pos4, out,
+):
+    nc = tc.nc
+    with ExitStack() as ctx:
+        lists = ctx.enter_context(tc.tile_pool(name="lists", bufs=1))
+        keep = ctx.enter_context(tc.tile_pool(name="keep", bufs=1))
+        ring = ctx.enter_context(tc.tile_pool(name="ring", bufs=2))
+        psum = ctx.enter_context(tc.psum_pool(name="psum", bufs=8))
+
+        def load_list(src, name):
+            tile = lists.tile(list(src.shape), U16, name=name)
+            nc.sync.dma_start(tile[:], src)
+            return tile
+
+        def load_w1(b, a):
+            raw = keep.tile([P, PACK, PASS], F32, name=f"w1raw{b}{a}")
+            rows = w1[a * PASS : (a + 1) * PASS, b * PASS : (b + 1) * PASS]
+            nc.sync.dma_start(raw[:], rows.rearrange("(p j) c -> p j c", j=PACK))
+            return raw
+
+        def load_table(a):
+            words = ring.tile([P, T], U32, name=f"tab{a}", tag="big", bufs=3, align_bytes=64)
+            nc.sync.dma_start(words[:].bitcast(I32), tab_words[a].rearrange("p t i -> p (t i)").bitcast(I32))
+            return words
+
+        def load_channels(src, name):
+            tile = keep.tile([P, H_PASSES, PACK], F32, name=name)
+            nc.scalar.dma_start(tile[:], src.rearrange("(b p t) -> p b t", p=P, t=PACK))
+            return tile
+
+        tab_planes = keep.tile([P, T], U8, name="tab_planes", align_bytes=64)
+        nc.vector.memset(tab_planes[:].bitcast(I32), 0)
+        w2_planes = keep.tile([P, H_PASSES, N], U8, name="w2_planes", align_bytes=64)
+        nc.vector.memset(w2_planes[:].rearrange("p a n -> p (a n)").bitcast(I32), 0)
+
+        raw = {}
+        for a in range(K_PASSES):
+            raw[0, a] = load_w1(0, a)
+            if a == 0:
+                for q in range(4):
+                    nc.sync.dma_start(
+                        tab_planes[32 * q : 32 * q + 4 * K_PASSES, :].bitcast(I32),
+                        tab_scales[:, 4 * q : 4 * q + 4, :].bitcast(I32),
+                    )
+        b1_t = load_channels(b1, "b1_t")
+        gain_t = load_channels(gain, "gain_t")
+        rest_t = load_channels(rest, "rest_t")
+        strain_t = load_channels(strain, "strain_t")
+        offs_t = load_list(offs, "offs_t")
+        table = [load_table(a) for a in range(K_PASSES)]
+        pos1_t = load_list(pos1, "pos1_t")
+        pos2_t = load_list(pos2, "pos2_t")
+        for a in range(K_PASSES):
+            raw[1, a] = load_w1(1, a)
+        w2_codes = keep.tile([P, H_PASSES, 2 * N], U8, name="w2_codes", align_bytes=64)
+        nc.sync.dma_start(w2_codes[:].bitcast(I32), w2_words.rearrange("a p n -> p a n").bitcast(I32))
+        for q in range(4):
+            nc.sync.dma_start(
+                w2_planes[32 * q : 32 * q + 4, :, :].bitcast(I32),
+                w2_scales[:, 4 * q : 4 * q + 4, :].rearrange("a r n -> r a n").bitcast(I32),
+            )
+        pos3_t = load_list(pos3, "pos3_t")
+        pos4_t = load_list(pos4, "pos4_t")
+
+        factors = []
+        for name, vec in (("f_rest", rest_t), ("f_strain", strain_t)):
+            col = keep.tile([P, H_PASSES * PACK], F32, name=name + "_col")
+            nc.vector.tensor_tensor(
+                col[:], gain_t[:].rearrange("p b t -> p (b t)"), vec[:].rearrange("p b t -> p (b t)"), ALU.mult
+            )
+            wide = keep.tile([P, H_PASSES * PACK, P1], F32, name=name)
+            nc.vector.tensor_copy(wide[:], col[:].unsqueeze(2).to_broadcast([P, H_PASSES * PACK, P1]))
+            factors.append(wide)
+
+        def quantise_w1(b, a):
+            grouped = ring.tile([P, PASS * PACK], BF16, name=f"w1bf{b}{a}", tag="w1bf", bufs=3, align_bytes=64)
+            nc.scalar.activation(
+                grouped[:].rearrange("p (t m j) -> p m j t", t=PACK, j=PACK),
+                raw[b, a][:].rearrange("p j (m t) -> p m j t", t=PACK),
+                ACT.Copy,
+            )
+            codes = keep.tile([P, PASS], U32, name=f"w1codes{b}{a}", align_bytes=64)
+            scales = keep.tile([P, PASS], U8, name=f"w1scales{b}{a}", align_bytes=64)
+            nc.vector.quantize_mx(out=codes[:].bitcast(FP8X4), scales=scales[:], in_=grouped[:])
+            return codes, scales
+
+        w1q = {}
+        for a in range(K_PASSES):
+            w1q[0, a] = quantise_w1(0, a)
+
+        picked_planes = keep.tile([P, S], U8, name="picked_planes", align_bytes=64)
+        nc.vector.tensor_copy(picked_planes[:], tab_planes[:].indirect(offs_t[:]))
+        picked = {}
+        for a in range(K_PASSES):
+            for h in range(HALVES):
+                words = keep.tile([P, BANK], U32, name=f"picked{a}{h}", align_bytes=64)
+                cols = BANK // 16
+                nc.vector.tensor_copy(words[:], table[a][:].indirect(offs_t[:, h * cols : (h + 1) * cols]))
+                picked[a, h] = words
+
+        def first_pass(bank, b, t, a, h):
+            codes, scales = w1q[b, a]
+            nc.tensor.matmul_mx(
+                out=bank[:],
+                lhsT=codes[:, t * P : (t + 1) * P].bitcast(FP8X4),
+                lhsT_scale=scales[:, t * P : (t + 1) * P],
+                rhs=picked[a, h][:].bitcast(FP8X4),
+                rhs_scale=picked_planes[4 * a : P, h * BANK : (h + 1) * BANK],
+                start=(a == 0),
+                stop=(a == K_PASSES - 1),
+            )
+
+        zq = []
+        for b in range(H_PASSES):
+            if b > 0:
+                for a in range(K_PASSES):
+                    w1q[b, a] = quantise_w1(b, a)
+            banks = {}
+            for t in range(PACK):
+                for h in range(HALVES):
+                    banks[t, h] = psum.tile([P, BANK], F32, name=f"d{b}{t}{h}", tag="bank")
+            for a in range(K_PASSES):
+                for t in range(PACK):
+                    for h in range(HALVES):
+                        first_pass(banks[t, h], b, t, a, h)
+            scaled = ring.tile([P, 2, PACK, P1], F32, name=f"scaled{b}", tag="big", bufs=3, align_bytes=64)
+            for t in range(PACK):
+                feat = ring.tile([P, S], F32, name=f"feat{b}{t}", tag="feat", bufs=6)
+                for h in range(HALVES):
+                    nc.scalar.activation(
+                        feat[:, h * BANK : (h + 1) * BANK], banks[t, h][:], ACT.Tanh, bias=b1_t[:, b, t : t + 1]
+                    )
+                for side, pos in enumerate((pos1_t, pos2_t)):
+                    nc.vector.tensor_tensor(
+                        scaled[:, side, t, :], feat[:].indirect(pos[:]), factors[side][:, b * PACK + t, :], ALU.mult
+                    )
+            z = ring.tile([P, P1 * PACK], BF16, name=f"z{b}", tag="z", align_bytes=64)
+            nc.vector.tensor_tensor(
+                z[:].rearrange("p (c i t) -> p c t i", i=4, t=PACK),
+                scaled[:, 0].rearrange("p t (c i) -> p c t i", i=4),
+                scaled[:, 1].rearrange("p t (c i) -> p c t i", i=4),
+                ALU.subtract,
+            )
+            z_codes = keep.tile([P, P1], U32, name=f"zcodes{b}", align_bytes=64)
+            z_scales = keep.tile([P, P1], U8, name=f"zscales{b}", align_bytes=64)
+            nc.vector.quantize_mx(out=z_codes[:].bitcast(FP8X4), scales=z_scales[:], in_=z[:])
+            zq.append((z_codes, z_scales))
+
+        ybanks = [psum.tile([P, BANK], F32, name=f"y{n}", tag="bank") for n in range(N_TILES)]
+        for b in range(H_PASSES):
+            for n in range(N_TILES):
+                nc.tensor.matmul_mx(
+                    out=ybanks[n][:],
+                    lhsT=w2_codes[:, b, 2 * n * P : 2 * (n + 1) * P].bitcast(FP4X4),
+                    lhsT_scale=w2_planes[:, b, n * P : (n + 1) * P],
+                    rhs=zq[b][0][:].bitcast(FP8X4),
+                    rhs_scale=zq[b][1][:],
+                    start=(b == 0),
+                    stop=(b == H_PASSES - 1),
+                )
+        for n in range(N_TILES):
+            y = ring.tile([P, P1], F32, name=f"ysb{n}", tag="feat", bufs=6)
+            nc.scalar.copy(y[:], ybanks[n][:])
+            pair = ring.tile([P, 2, P2], F32, name=f"pair{n}", tag="pair", bufs=2)
+            nc.vector.tensor_copy(pair[:, 0, :], y[:].indirect(pos3_t[:]))
+            nc.vector.tensor_copy(pair[:, 1, :], y[:].indirect(pos4_t[:]))
+            best = keep.tile([P, P2], F32, name=f"best{n}")
+            nc.vector.tensor_tensor(best[:], pair[:, 0, :], pair[:, 1, :], ALU.max)
+            nc.sync.dma_start(out[n * P : (n + 1) * P, :], best[:])

@@ -35,7 +35,7 @@ def tile_list_ewe_posture_contrast_kernel(
         lists = ctx.enter_context(tc.tile_pool(name="lists", bufs=1))
         keep = ctx.enter_context(tc.tile_pool(name="keep", bufs=1))
         ring = ctx.enter_context(tc.tile_pool(name="ring", bufs=2))
-        psum = ctx.enter_context(tc.psum_pool(name="psum", bufs=8))
+        psum = ctx.enter_context(tc.psum_pool(name="psum", bufs=1))
 
         def load_list(src, name):
             tile = lists.tile(list(src.shape), U16, name=name)
@@ -59,19 +59,18 @@ def tile_list_ewe_posture_contrast_kernel(
             return tile
 
         tab_planes = keep.tile([P, T], U8, name="tab_planes", align_bytes=64)
-        nc.vector.memset(tab_planes[:].bitcast(I32), 0)
+        nc.gpsimd.memset(tab_planes[:].bitcast(I32), 0)
+        for q in range(4):
+            nc.gpsimd.dma_start(
+                tab_planes[32 * q : 32 * q + 4 * K_PASSES, :].bitcast(I32),
+                tab_scales[:, 4 * q : 4 * q + 4, :].bitcast(I32),
+            )
         w2_planes = keep.tile([P, H_PASSES, N], U8, name="w2_planes", align_bytes=64)
         nc.vector.memset(w2_planes[:].rearrange("p a n -> p (a n)").bitcast(I32), 0)
 
         raw = {}
         for a in range(K_PASSES):
             raw[0, a] = load_w1(0, a)
-            if a == 0:
-                for q in range(4):
-                    nc.sync.dma_start(
-                        tab_planes[32 * q : 32 * q + 4 * K_PASSES, :].bitcast(I32),
-                        tab_scales[:, 4 * q : 4 * q + 4, :].bitcast(I32),
-                    )
         b1_t = load_channels(b1, "b1_t")
         gain_t = load_channels(gain, "gain_t")
         rest_t = load_channels(rest, "rest_t")
@@ -102,21 +101,23 @@ def tile_list_ewe_posture_contrast_kernel(
             nc.vector.tensor_copy(wide[:], col[:].unsqueeze(2).to_broadcast([P, H_PASSES * PACK, P1]))
             factors.append(wide)
 
-        def quantise_w1(b, a):
-            grouped = ring.tile([P, PASS * PACK], BF16, name=f"w1bf{b}{a}", tag="w1bf", bufs=3, align_bytes=64)
+        def quantise_w1(b, a, grouped):
             nc.scalar.activation(
-                grouped[:].rearrange("p (t m j) -> p m j t", t=PACK, j=PACK),
+                grouped.rearrange("p (t m j) -> p m j t", t=PACK, j=PACK),
                 raw[b, a][:].rearrange("p j (m t) -> p m j t", t=PACK),
                 ACT.Copy,
             )
             codes = keep.tile([P, PASS], U32, name=f"w1codes{b}{a}", align_bytes=64)
             scales = keep.tile([P, PASS], U8, name=f"w1scales{b}{a}", align_bytes=64)
-            nc.vector.quantize_mx(out=codes[:].bitcast(FP8X4), scales=scales[:], in_=grouped[:])
-            return codes, scales
+            nc.vector.quantize_mx(out=codes[:].bitcast(FP8X4), scales=scales[:], in_=grouped)
+            w1q[b, a] = (codes, scales)
+
+        def staging(name, tag):
+            return ring.tile([P, PASS * PACK], BF16, name=name, tag=tag, bufs=1, align_bytes=64)
 
         w1q = {}
         for a in range(K_PASSES):
-            w1q[0, a] = quantise_w1(0, a)
+            quantise_w1(0, a, staging(f"w1bf0{a}", f"stage{a}")[:])
 
         picked_planes = keep.tile([P, S], U8, name="picked_planes", align_bytes=64)
         nc.vector.tensor_copy(picked_planes[:], tab_planes[:].indirect(offs_t[:]))
@@ -128,72 +129,106 @@ def tile_list_ewe_posture_contrast_kernel(
                 nc.vector.tensor_copy(words[:], table[a][:].indirect(offs_t[:, h * cols : (h + 1) * cols]))
                 picked[a, h] = words
 
-        def first_pass(bank, b, t, a, h):
-            codes, scales = w1q[b, a]
-            nc.tensor.matmul_mx(
-                out=bank[:],
-                lhsT=codes[:, t * P : (t + 1) * P].bitcast(FP8X4),
-                lhsT_scale=scales[:, t * P : (t + 1) * P],
-                rhs=picked[a, h][:].bitcast(FP8X4),
-                rhs_scale=picked_planes[4 * a : P, h * BANK : (h + 1) * BANK],
-                start=(a == 0),
-                stop=(a == K_PASSES - 1),
-            )
+        def bank_tile(name, index):
+            return psum.tile([P, BANK], F32, name=name, tag=f"bank{index}")
 
-        zq = []
-        for b in range(H_PASSES):
-            if b > 0:
-                for a in range(K_PASSES):
-                    w1q[b, a] = quantise_w1(b, a)
+        def first_product(b, slots, first_bank):
             banks = {}
-            for t in range(PACK):
+            for i, t in enumerate(slots):
                 for h in range(HALVES):
-                    banks[t, h] = psum.tile([P, BANK], F32, name=f"d{b}{t}{h}", tag="bank")
+                    banks[t, h] = bank_tile(f"d{b}{t}{h}", first_bank + HALVES * i + h)
             for a in range(K_PASSES):
-                for t in range(PACK):
+                codes, scales = w1q[b, a]
+                for t in slots:
                     for h in range(HALVES):
-                        first_pass(banks[t, h], b, t, a, h)
-            scaled = ring.tile([P, 2, PACK, P1], F32, name=f"scaled{b}", tag="big", bufs=3, align_bytes=64)
-            for t in range(PACK):
+                        nc.tensor.matmul_mx(
+                            out=banks[t, h][:],
+                            lhsT=codes[:, t * P : (t + 1) * P].bitcast(FP8X4),
+                            lhsT_scale=scales[:, t * P : (t + 1) * P],
+                            rhs=picked[a, h][:].bitcast(FP8X4),
+                            rhs_scale=picked_planes[4 * a : P, h * BANK : (h + 1) * BANK],
+                            start=(a == 0),
+                            stop=(a == K_PASSES - 1),
+                        )
+            for t in slots:
                 feat = ring.tile([P, S], F32, name=f"feat{b}{t}", tag="feat", bufs=6)
                 for h in range(HALVES):
                     nc.scalar.activation(
                         feat[:, h * BANK : (h + 1) * BANK], banks[t, h][:], ACT.Tanh, bias=b1_t[:, b, t : t + 1]
                     )
-                for side, pos in enumerate((pos1_t, pos2_t)):
-                    nc.vector.tensor_tensor(
-                        scaled[:, side, t, :], feat[:].indirect(pos[:]), factors[side][:, b * PACK + t, :], ALU.mult
-                    )
-            z = ring.tile([P, P1 * PACK], BF16, name=f"z{b}", tag="z", align_bytes=64)
+                feats[b, t] = feat
+
+        def pick_pairs(b, t, scaled):
+            for side, pos in enumerate((pos1_t, pos2_t)):
+                at = (2 * t + side) * P1
+                nc.vector.tensor_tensor(
+                    scaled[:, at : at + P1], feats[b, t][:].indirect(pos[:]), factors[side][:, b * PACK + t, :], ALU.mult
+                )
+
+        def contrast(name, scaled, z, lo, width):
+            sides = scaled[:].rearrange("p (t s m) -> p s t m", t=PACK, s=2)
             nc.vector.tensor_tensor(
-                z[:].rearrange("p (c i t) -> p c t i", i=4, t=PACK),
-                scaled[:, 0].rearrange("p t (c i) -> p c t i", i=4),
-                scaled[:, 1].rearrange("p t (c i) -> p c t i", i=4),
+                z.rearrange("p (c i t) -> p c t i", i=4, t=PACK),
+                sides[:, 0, :, lo : lo + width].rearrange("p t (c i) -> p c t i", i=4),
+                sides[:, 1, :, lo : lo + width].rearrange("p t (c i) -> p c t i", i=4),
                 ALU.subtract,
             )
-            z_codes = keep.tile([P, P1], U32, name=f"zcodes{b}", align_bytes=64)
-            z_scales = keep.tile([P, P1], U8, name=f"zscales{b}", align_bytes=64)
-            nc.vector.quantize_mx(out=z_codes[:].bitcast(FP8X4), scales=z_scales[:], in_=z[:])
-            zq.append((z_codes, z_scales))
+            codes = keep.tile([P, width], U32, name=name + "codes", align_bytes=64)
+            scales = keep.tile([P, width], U8, name=name + "scales", align_bytes=64)
+            nc.vector.quantize_mx(out=codes[:].bitcast(FP8X4), scales=scales[:], in_=z)
+            return codes, scales
 
-        ybanks = [psum.tile([P, BANK], F32, name=f"y{n}", tag="bank") for n in range(N_TILES)]
-        for b in range(H_PASSES):
-            for n in range(N_TILES):
-                nc.tensor.matmul_mx(
-                    out=ybanks[n][:],
-                    lhsT=w2_codes[:, b, 2 * n * P : 2 * (n + 1) * P].bitcast(FP4X4),
-                    lhsT_scale=w2_planes[:, b, n * P : (n + 1) * P],
-                    rhs=zq[b][0][:].bitcast(FP8X4),
-                    rhs_scale=zq[b][1][:],
-                    start=(b == 0),
-                    stop=(b == H_PASSES - 1),
-                )
-        for n in range(N_TILES):
-            y = ring.tile([P, P1], F32, name=f"ysb{n}", tag="feat", bufs=6)
-            nc.scalar.copy(y[:], ybanks[n][:])
-            pair = ring.tile([P, 2, P2], F32, name=f"pair{n}", tag="pair", bufs=2)
-            nc.vector.tensor_copy(pair[:, 0, :], y[:].indirect(pos3_t[:]))
-            nc.vector.tensor_copy(pair[:, 1, :], y[:].indirect(pos4_t[:]))
-            best = keep.tile([P, P2], F32, name=f"best{n}")
-            nc.vector.tensor_tensor(best[:], pair[:, 0, :], pair[:, 1, :], ALU.max)
-            nc.sync.dma_start(out[n * P : (n + 1) * P, :], best[:])
+        feats = {}
+        zq = {}
+        half = P1 // 2
+        first_product(0, range(PACK), 0)
+        scaled0 = ring.tile([P, 2 * PACK * P1], F32, name="scaled0", tag="big", bufs=3, align_bytes=64)
+        for t in range(PACK - 1):
+            pick_pairs(0, t, scaled0)
+        quantise_w1(1, 0, scaled0[:, 2 * (PACK - 1) * P1 :].bitcast(BF16))
+        pick_pairs(0, PACK - 1, scaled0)
+        quantise_w1(1, 1, staging("w1bf11", "stage1")[:])
+        quantise_w1(1, 2, staging("w1bf12", "stage2")[:])
+        codes, scales = contrast("z0", scaled0, staging("z0", "stage2")[:], 0, P1)
+        for h in range(2):
+            zq[0, h] = (codes[:, h * half : (h + 1) * half], scales[:, h * half : (h + 1) * half])
+
+        scaled1 = ring.tile([P, 2 * PACK * P1], F32, name="scaled1", tag="big", bufs=3, align_bytes=64)
+        for slots in ((0, 1), (2, 3)):
+            first_product(1, slots, 0)
+            for t in slots:
+                pick_pairs(1, t, scaled1)
+        z1 = staging("z1", "stage0")
+        for h in range(2):
+            codes, scales = contrast(f"z1{h}", scaled1, z1[:, h * half * PACK : (h + 1) * half * PACK], h * half, half)
+            zq[1, h] = (codes[:], scales[:])
+
+        ysb = [ring.tile([P, P1], F32, name=f"ysb{n}", tag="feat", bufs=6) for n in range(N_TILES)]
+        for i in range(N_TILES // 2):
+            for h in range(2):
+                bank = bank_tile(f"y{h}{i}", (4 + 2 * i + h) % 8)
+                for b in range(H_PASSES):
+                    for u in range(2):
+                        n = 2 * i + u
+                        nc.tensor.matmul_mx(
+                            out=bank[:, u * half : (u + 1) * half],
+                            lhsT=w2_codes[:, b, 2 * n * P : 2 * (n + 1) * P].bitcast(FP4X4),
+                            lhsT_scale=w2_planes[:, b, n * P : (n + 1) * P],
+                            rhs=zq[b, h][0].bitcast(FP8X4),
+                            rhs_scale=zq[b, h][1],
+                            start=(b == 0 and u == 0),
+                            stop=(b == H_PASSES - 1 and u == 1),
+                        )
+                for u in range(2):
+                    nc.scalar.copy(ysb[2 * i + u][:, h * half : (h + 1) * half], bank[:, u * half : (u + 1) * half])
+        pairs = []
+        for n in range(N_TILES + 1):
+            if n < N_TILES:
+                pair = ring.tile([P, 2, P2], F32, name=f"pair{n}", tag="pair", bufs=3)
+                nc.vector.tensor_copy(pair[:, 0, :], ysb[n][:].indirect(pos3_t[:]))
+                nc.vector.tensor_copy(pair[:, 1, :], ysb[n][:].indirect(pos4_t[:]))
+                pairs.append(pair)
+            if n > 0:
+                best = keep.tile([P, P2], F32, name=f"best{n - 1}")
+                nc.vector.tensor_tensor(best[:], pairs[n - 1][:, 0, :], pairs[n - 1][:, 1, :], ALU.max)
+                nc.sync.dma_start(out[(n - 1) * P : n * P, :], best[:])

from contextlib import ExitStack

import concourse.mybir as mybir

K, H, N, T, S, P1, P2 = 1536, 1024, 768, 4096, 1024, 512, 256
FLOPS = 2 * K * H * S + 2 * H * N * P1

F32 = mybir.dt.float32
BF16 = mybir.dt.bfloat16
I32 = mybir.dt.int32
U32 = mybir.dt.uint32
U16 = mybir.dt.uint16
U8 = mybir.dt.uint8
FP8X4 = mybir.dt.float8_e4m3fn_x4
FP4X4 = mybir.dt.float4_e2m1fn_x4
ALU = mybir.AluOpType
ACT = mybir.ActivationFunctionType

P = 128
PACK = 4
PASS = P * PACK
BANK = 512
K_PASSES = K // PASS
H_PASSES = H // PASS
HALVES = S // BANK
N_TILES = N // P


def tile_list_ewe_posture_contrast_kernel(
    tc, tab_words, tab_scales, offs, w1, b1, gain, pos1, pos2, rest, strain,
    w2_words, w2_scales, pos3, pos4, out,
):
    nc = tc.nc
    with ExitStack() as ctx:
        lists = ctx.enter_context(tc.tile_pool(name="lists", bufs=1))
        keep = ctx.enter_context(tc.tile_pool(name="keep", bufs=1))
        ring = ctx.enter_context(tc.tile_pool(name="ring", bufs=2))
        psum = ctx.enter_context(tc.psum_pool(name="psum", bufs=1))

        def load_list(src, name):
            tile = lists.tile(list(src.shape), U16, name=name)
            nc.sync.dma_start(tile[:], src)
            return tile

        def load_w1(b, a):
            raw = keep.tile([P, PACK, PASS], F32, name=f"w1raw{b}{a}")
            rows = w1[a * PASS : (a + 1) * PASS, b * PASS : (b + 1) * PASS]
            nc.sync.dma_start(raw[:], rows.rearrange("(p j) c -> p j c", j=PACK))
            return raw

        def load_table(a):
            words = ring.tile([P, T], U32, name=f"tab{a}", tag="big", bufs=3, align_bytes=64)
            nc.sync.dma_start(words[:].bitcast(I32), tab_words[a].rearrange("p t i -> p (t i)").bitcast(I32))
            return words

        def load_channels(src, name):
            tile = keep.tile([P, H_PASSES, PACK], F32, name=name)
            nc.scalar.dma_start(tile[:], src.rearrange("(b p t) -> p b t", p=P, t=PACK))
            return tile

        tab_planes = keep.tile([P, T], U8, name="tab_planes", align_bytes=64)
        nc.gpsimd.memset(tab_planes[:].bitcast(I32), 0)
        for q in range(4):
            nc.gpsimd.dma_start(
                tab_planes[32 * q : 32 * q + 4 * K_PASSES, :].bitcast(I32),
                tab_scales[:, 4 * q : 4 * q + 4, :].bitcast(I32),
            )
        w2_planes = keep.tile([P, H_PASSES, N], U8, name="w2_planes", align_bytes=64)
        nc.vector.memset(w2_planes[:].rearrange("p a n -> p (a n)").bitcast(I32), 0)

        raw = {}
        for a in range(K_PASSES):
            raw[0, a] = load_w1(0, a)
        b1_t = load_channels(b1, "b1_t")
        gain_t = load_channels(gain, "gain_t")
        rest_t = load_channels(rest, "rest_t")
        strain_t = load_channels(strain, "strain_t")
        offs_t = load_list(offs, "offs_t")
        table = [load_table(a) for a in range(K_PASSES)]
        pos1_t = load_list(pos1, "pos1_t")
        pos2_t = load_list(pos2, "pos2_t")
        for a in range(K_PASSES):
            raw[1, a] = load_w1(1, a)
        w2_codes = keep.tile([P, H_PASSES, 2 * N], U8, name="w2_codes", align_bytes=64)
        nc.sync.dma_start(w2_codes[:].bitcast(I32), w2_words.rearrange("a p n -> p a n").bitcast(I32))
        for q in range(4):
            nc.sync.dma_start(
                w2_planes[32 * q : 32 * q + 4, :, :].bitcast(I32),
                w2_scales[:, 4 * q : 4 * q + 4, :].rearrange("a r n -> r a n").bitcast(I32),
            )
        pos3_t = load_list(pos3, "pos3_t")
        pos4_t = load_list(pos4, "pos4_t")

        factors = []
        for name, vec in (("f_rest", rest_t), ("f_strain", strain_t)):
            col = keep.tile([P, H_PASSES * PACK], F32, name=name + "_col")
            nc.vector.tensor_tensor(
                col[:], gain_t[:].rearrange("p b t -> p (b t)"), vec[:].rearrange("p b t -> p (b t)"), ALU.mult
            )
            wide = keep.tile([P, H_PASSES * PACK, P1], F32, name=name)
            nc.vector.tensor_copy(wide[:], col[:].unsqueeze(2).to_broadcast([P, H_PASSES * PACK, P1]))
            factors.append(wide)

        def quantise_w1(b, a, grouped):
            nc.scalar.activation(
                grouped.rearrange("p (t m j) -> p m j t", t=PACK, j=PACK),
                raw[b, a][:].rearrange("p j (m t) -> p m j t", t=PACK),
                ACT.Copy,
            )
            codes = keep.tile([P, PASS], U32, name=f"w1codes{b}{a}", align_bytes=64)
            scales = keep.tile([P, PASS], U8, name=f"w1scales{b}{a}", align_bytes=64)
            nc.vector.quantize_mx(out=codes[:].bitcast(FP8X4), scales=scales[:], in_=grouped)
            w1q[b, a] = (codes, scales)

        def staging(name, tag):
            return ring.tile([P, PASS * PACK], BF16, name=name, tag=tag, bufs=1, align_bytes=64)

        w1q = {}
        for a in range(K_PASSES):
            quantise_w1(0, a, staging(f"w1bf0{a}", f"stage{a}")[:])

        picked_planes = keep.tile([P, S], U8, name="picked_planes", align_bytes=64)
        nc.vector.tensor_copy(picked_planes[:], tab_planes[:].indirect(offs_t[:]))
        picked = {}
        for a in range(K_PASSES):
            for h in range(HALVES):
                words = keep.tile([P, BANK], U32, name=f"picked{a}{h}", align_bytes=64)
                cols = BANK // 16
                nc.vector.tensor_copy(words[:], table[a][:].indirect(offs_t[:, h * cols : (h + 1) * cols]))
                picked[a, h] = words

        def bank_tile(name, index):
            return psum.tile([P, BANK], F32, name=name, tag=f"bank{index}")

        def first_product(b, slots, first_bank):
            banks = {}
            for i, t in enumerate(slots):
                for h in range(HALVES):
                    banks[t, h] = bank_tile(f"d{b}{t}{h}", first_bank + HALVES * i + h)
            for a in range(K_PASSES):
                codes, scales = w1q[b, a]
                for t in slots:
                    for h in range(HALVES):
                        nc.tensor.matmul_mx(
                            out=banks[t, h][:],
                            lhsT=codes[:, t * P : (t + 1) * P].bitcast(FP8X4),
                            lhsT_scale=scales[:, t * P : (t + 1) * P],
                            rhs=picked[a, h][:].bitcast(FP8X4),
                            rhs_scale=picked_planes[4 * a : P, h * BANK : (h + 1) * BANK],
                            start=(a == 0),
                            stop=(a == K_PASSES - 1),
                        )
            for t in slots:
                feat = ring.tile([P, S], F32, name=f"feat{b}{t}", tag="feat", bufs=6)
                for h in range(HALVES):
                    nc.scalar.activation(
                        feat[:, h * BANK : (h + 1) * BANK], banks[t, h][:], ACT.Tanh, bias=b1_t[:, b, t : t + 1]
                    )
                feats[b, t] = feat

        def pick_pairs(b, t, scaled):
            for side, pos in enumerate((pos1_t, pos2_t)):
                at = (2 * t + side) * P1
                nc.vector.tensor_tensor(
                    scaled[:, at : at + P1], feats[b, t][:].indirect(pos[:]), factors[side][:, b * PACK + t, :], ALU.mult
                )

        def contrast(name, scaled, z, lo, width):
            sides = scaled[:].rearrange("p (t s m) -> p s t m", t=PACK, s=2)
            nc.vector.tensor_tensor(
                z.rearrange("p (c i t) -> p c t i", i=4, t=PACK),
                sides[:, 0, :, lo : lo + width].rearrange("p t (c i) -> p c t i", i=4),
                sides[:, 1, :, lo : lo + width].rearrange("p t (c i) -> p c t i", i=4),
                ALU.subtract,
            )
            codes = keep.tile([P, width], U32, name=name + "codes", align_bytes=64)
            scales = keep.tile([P, width], U8, name=name + "scales", align_bytes=64)
            nc.vector.quantize_mx(out=codes[:].bitcast(FP8X4), scales=scales[:], in_=z)
            return codes, scales

        feats = {}
        zq = {}
        half = P1 // 2
        first_product(0, range(PACK), 0)
        scaled0 = ring.tile([P, 2 * PACK * P1], F32, name="scaled0", tag="big", bufs=3, align_bytes=64)
        for t in range(PACK - 1):
            pick_pairs(0, t, scaled0)
        quantise_w1(1, 0, scaled0[:, 2 * (PACK - 1) * P1 :].bitcast(BF16))
        pick_pairs(0, PACK - 1, scaled0)
        quantise_w1(1, 1, staging("w1bf11", "stage1")[:])
        quantise_w1(1, 2, staging("w1bf12", "stage2")[:])
        codes, scales = contrast("z0", scaled0, staging("z0", "stage2")[:], 0, P1)
        for h in range(2):
            zq[0, h] = (codes[:, h * half : (h + 1) * half], scales[:, h * half : (h + 1) * half])

        scaled1 = ring.tile([P, 2 * PACK * P1], F32, name="scaled1", tag="big", bufs=3, align_bytes=64)
        for slots in ((0, 1), (2, 3)):
            first_product(1, slots, 0)
            for t in slots:
                pick_pairs(1, t, scaled1)
        z1 = staging("z1", "stage0")
        for h in range(2):
            codes, scales = contrast(f"z1{h}", scaled1, z1[:, h * half * PACK : (h + 1) * half * PACK], h * half, half)
            zq[1, h] = (codes[:], scales[:])

        ysb = [ring.tile([P, P1], F32, name=f"ysb{n}", tag="feat", bufs=6) for n in range(N_TILES)]
        for i in range(N_TILES // 2):
            for h in range(2):
                bank = bank_tile(f"y{h}{i}", (4 + 2 * i + h) % 8)
                for b in range(H_PASSES):
                    for u in range(2):
                        n = 2 * i + u
                        nc.tensor.matmul_mx(
                            out=bank[:, u * half : (u + 1) * half],
                            lhsT=w2_codes[:, b, 2 * n * P : 2 * (n + 1) * P].bitcast(FP4X4),
                            lhsT_scale=w2_planes[:, b, n * P : (n + 1) * P],
                            rhs=zq[b, h][0].bitcast(FP8X4),
                            rhs_scale=zq[b, h][1],
                            start=(b == 0 and u == 0),
                            stop=(b == H_PASSES - 1 and u == 1),
                        )
                for u in range(2):
                    nc.scalar.copy(ysb[2 * i + u][:, h * half : (h + 1) * half], bank[:, u * half : (u + 1) * half])
        pairs = []
        for n in range(N_TILES + 1):
            if n < N_TILES:
                pair = ring.tile([P, 2, P2], F32, name=f"pair{n}", tag="pair", bufs=3)
                nc.vector.tensor_copy(pair[:, 0, :], ysb[n][:].indirect(pos3_t[:]))
                nc.vector.tensor_copy(pair[:, 1, :], ysb[n][:].indirect(pos4_t[:]))
                pairs.append(pair)
            if n > 0:
                best = keep.tile([P, P2], F32, name=f"best{n - 1}")
                nc.vector.tensor_tensor(best[:], pairs[n - 1][:, 0, :], pairs[n - 1][:, 1, :], ALU.max)
                nc.sync.dma_start(out[(n - 1) * P : n * P, :], best[:])
